import numpy as np
import ml_dtypes


def mxq(x, axis, fmt="e4m3"):
    dtype, down = {"e4m3": (ml_dtypes.float8_e4m3fn, 7), "e5m2": (ml_dtypes.float8_e5m2, 14)}[fmt]
    v = np.moveaxis(np.asarray(x, np.float32).astype(ml_dtypes.bfloat16).astype(np.float64), axis, -1)
    blocks = v.reshape(v.shape[:-1] + (-1, 32))
    amax = np.abs(blocks).max(-1, keepdims=True)
    byte = np.maximum(np.where(amax > 0, np.frexp(amax)[1] - 1 + 127, 0) - down, 1)
    scale = np.exp2(byte - 127.0)
    codes = (blocks / scale).astype(np.float32).astype(dtype).astype(np.float64)
    return np.moveaxis((codes * scale).reshape(v.shape), -1, axis)


WIDE = False


def mx_kscale(k):
    if not WIDE:
        return np.ones(k)
    levels = np.array([10, -10, 5, -5, 0])
    if k % 512:
        return np.exp2(np.random.permutation(np.resize(levels, k // 32))).repeat(32)
    a = np.empty((k // 512, 16))
    for p in range(k // 512):
        a[p, :8] = np.random.permutation(np.resize(levels, 8))
        for g in range(8):
            far = levels[np.abs(levels - a[p, g]) >= 10]
            a[p, g + 8] = far[np.random.randint(len(far))]
    return np.exp2(a.ravel()).repeat(32)


def f64(x):
    return np.asarray(x).astype(np.float64)


def striped(idx):
    return np.tile(idx.reshape(-1, 16).T, (8, 1)).astype(np.uint16)


def unstriped(offs):
    return offs[:16].T.reshape(-1).astype(np.int64)


def pack_weight(w):
    k, n = w.shape
    w = f64(np.asarray(w, np.float32).astype(ml_dtypes.bfloat16)).reshape(k // 32, 32, n)
    amax = np.abs(w).max(1)
    byte = np.clip(np.where(amax > 0, np.frexp(amax)[1] - 1 + 127 - 7, 1), 1, 254)
    scaled = (w * np.exp2(127.0 - byte)[:, None, :]).reshape(k, n).astype(np.float32)
    words = np.ascontiguousarray(scaled.reshape(k // 512, 128, 4, n).transpose(0, 1, 3, 2)).astype(ml_dtypes.float8_e4m3fn).view(np.uint8)
    return words, np.ascontiguousarray(byte.astype(np.uint8).reshape(k // 512, 16, n))


def unpack_weight(words, scales):
    g, p, n, _ = words.shape
    vals = np.ascontiguousarray(words).view(ml_dtypes.float8_e4m3fn).astype(np.float64) * np.repeat(np.exp2(scales.astype(np.float64) - 127.0), 8, axis=1)[..., None]
    return vals.transpose(0, 1, 3, 2).reshape(g * 512, n)


E2M1 = np.array([0.0, 0.5, 1.0, 1.5, 2.0, 3.0, 4.0, 6.0, -0.0, -0.5, -1.0, -1.5, -2.0, -3.0, -4.0, -6.0])


def pack_fp4(w):
    k, n = w.shape
    w = f64(np.asarray(w, np.float32).astype(ml_dtypes.bfloat16)).reshape(k // 32, 32, n)
    amax = np.abs(w).max(1)
    mant, ex = np.frexp(amax / 6.0)
    byte = np.clip(np.where(amax > 0, np.where(mant > 0.5, ex, ex - 1) + 127, 1), 1, 254)
    scaled = (w * np.exp2(127.0 - byte)[:, None, :]).reshape(k, n).astype(np.float32)
    c = np.ascontiguousarray(scaled.reshape(k // 512, 128, 4, n).transpose(0, 1, 3, 2)).astype(ml_dtypes.float4_e2m1fn).view(np.uint8) & 0xF
    words = (c[..., 0::2] | (c[..., 1::2] << 4)).reshape(k // 512, 128, 2 * n)
    return np.ascontiguousarray(words), np.ascontiguousarray(byte.astype(np.uint8).reshape(k // 512, 16, n))


def unpack_fp4(words, scales):
    g, _, n = scales.shape
    words = np.ascontiguousarray(words).reshape(g, 128, n, 2)
    nib = np.empty((g, 128, n, 4), np.uint8)
    nib[..., 0::2] = words & 0xF
    nib[..., 1::2] = words >> 4
    vals = E2M1[nib] * np.repeat(np.exp2(scales.astype(np.float64) - 127.0), 8, axis=1)[..., None]
    return vals.transpose(0, 1, 3, 2).reshape(g * 512, n)


K, T, S, N, H = 1024, 1024, 512, 128, 512


def setup_inputs():
    n = np.random.standard_normal
    s = mx_kscale(K)[:, None]
    u = mx_kscale(H)
    packed_xT = pack_weight(n((K, T)) * s)
    packed_w1 = pack_fp4(n((K, H)) / np.sqrt(K) / s)
    packed_w2 = pack_fp4(n((H, N)) / np.sqrt(H) / u[:, None])
    return {
        "x_words": packed_xT[0],
        "x_scales": packed_xT[1],
        "w1_words": packed_w1[0],
        "w1_scales": packed_w1[1],
        "unit": (np.random.uniform(0.6, 1.4, (H, 1)) * u[:, None]).astype(np.float32),
        "w2_words": packed_w2[0],
        "w2_scales": packed_w2[1],
        "offs": striped(np.random.permutation(T)[:S]),
        "p1": striped(np.random.permutation(S)),
        "p2": striped(np.random.permutation(S)),
        "p3": striped(np.random.permutation(S)),
    }


def reference(x_words, x_scales, w1_words, w1_scales, unit, w2_words, w2_scales, offs, p1, p2, p3):
    xq = unpack_weight(x_words, x_scales)[:, unstriped(offs)]
    y = unpack_fp4(w1_words, w1_scales).T @ xq
    y2 = (y) ** 2
    ms = y2.mean(axis=1, keepdims=True)
    nrm = y / np.sqrt(ms + 0.1)
    a1 = nrm[:, unstriped(p1)]
    a2 = nrm[:, unstriped(p2)]
    a3 = nrm[:, unstriped(p3)]
    sum3 = a1 + a2 + a3
    mxp = np.maximum(np.maximum(a1, a2), a3)
    mnp = np.minimum(np.minimum(a1, a2), a3)
    med = sum3 - mxp - mnp
    hid = f64(unit) * (med * np.abs(nrm) - (0.4 * (mxp - mnp)))
    return unpack_fp4(w2_words, w2_scales).T @ mxq(hid, 0, "e4m3")

@@ -1,0 +1,226 @@
+from contextlib import ExitStack
+
+import concourse.mybir as mybir
+
+K, T, S, N, H = 1024, 1024, 512, 128, 512
+FLOPS = 2 * K * H * S + 2 * H * N * S
+
+F32 = mybir.dt.float32
+BF16 = mybir.dt.bfloat16
+I32 = mybir.dt.int32
+U32 = mybir.dt.uint32
+U16 = mybir.dt.uint16
+U8 = mybir.dt.uint8
+FP8X4 = mybir.dt.float8_e4m3fn_x4
+FP4X4 = mybir.dt.float4_e2m1fn_x4
+ALU = mybir.AluOpType
+ACT = mybir.ActivationFunctionType
+
+P = 128
+PACK = 4
+PASSES = K // (P * PACK)
+HALF = S // 2
+QUARTER = S // 4
+
+
+def tile_picked_ygossip_rng_p_kernel(
+    tc, x_words, x_scales, w1_words, w1_scales, unit, w2_words, w2_scales, offs, p1, p2, p3, out
+):
+    nc = tc.nc
+    with ExitStack() as ctx:
+        keep = ctx.enter_context(tc.tile_pool(name="keep", bufs=1))
+        psum = ctx.enter_context(tc.psum_pool(name="psum", bufs=1))
+
+        def sb(name, shape, dtype):
+            return keep.tile(shape, dtype, name=name, align_bytes=64)
+
+        def load_scale_rows(queue, plane, rows):
+            for q in range(4):
+                queue.dma_start(
+                    plane[32 * q : 32 * q + 4].bitcast(I32),
+                    rows[:, 4 * q : 4 * q + 4, :].rearrange("o r c -> r o c").bitcast(I32),
+                )
+
+        xs = sb("xs", [P, PASSES, T], U8)
+        w1s = sb("w1s", [P, PASSES, H], U8)
+        w2s = sb("w2s", [P, 1, N], U8)
+        nc.vector.memset(xs[:].bitcast(I32), 0)
+        nc.gpsimd.memset(w1s[:].bitcast(I32), 0)
+        nc.gpsimd.memset(w2s[:].bitcast(I32), 0)
+
+        pick = keep.tile([P, S // 16], U16, name="pick")
+        nc.sync.dma_start(pick[:], offs)
+        w1w = sb("w1w", [P, PASSES, 2 * H], U8)
+        nc.sync.dma_start(w1w[:].bitcast(I32), w1_words.rearrange("o p c -> p o c").bitcast(I32))
+        xw = sb("xw", [P, PASSES, T], U32)
+        nc.sync.dma_start(xw[:].bitcast(I32), x_words.rearrange("o p n t -> p o (n t)").bitcast(I32))
+        load_scale_rows(nc.scalar, xs, x_scales)
+        load_scale_rows(nc.scalar, w1s, w1_scales)
+        lists = []
+        for name, src in (("la", p1), ("lc", p3), ("lb", p2)):
+            lst = keep.tile([P, S // 16], U16, name=name)
+            nc.sync.dma_start(lst[:], src)
+            lists.append(lst)
+        u = sb("u", [P, PACK], F32)
+        nc.sync.dma_start(u[:], unit.rearrange("(p t) o -> p (t o)", t=PACK))
+        w2w = sb("w2w", [P, 2 * N], U8)
+        nc.sync.dma_start(w2w[:].bitcast(I32), w2_words[0].bitcast(I32))
+        load_scale_rows(nc.sync, w2s, w2_scales)
+
+        w1wd = [sb("w1wd%d" % t, [P, PASSES, 2 * P], U8) for t in range(PACK)]
+        w1sd = [sb("w1sd%d" % t, [P, PASSES, P], U8) for t in range(PACK)]
+        for t in range(PACK):
+            nc.gpsimd.tensor_copy(
+                w1wd[t][:].rearrange("p o (m b) -> p o m b", b=2),
+                w1w[:].rearrange("p o (m t b) -> p o m t b", t=PACK, b=2)[:, :, :, t, :],
+            )
+            nc.gpsimd.tensor_copy(w1sd[t][:], w1s[:].rearrange("p o (m t) -> p o m t", t=PACK)[:, :, :, t])
+        um = sb("um", [P, PACK], F32)
+        nc.gpsimd.tensor_scalar(um[:], u[:], -0.4, 0.0, ALU.mult, ALU.add)
+        expo = sb("expo", [P, PACK], F32)
+        nc.gpsimd.memset(expo[:], -0.5)
+
+        gw = [sb("gw%d" % o, [P, S], U32) for o in range(PASSES)]
+        gs = [sb("gs%d" % o, [P, S], U8) for o in range(PASSES)]
+        for o in range(PASSES):
+            nc.vector.tensor_copy(gs[o][:], xs[:, o, :].indirect(pick[:]))
+        for o in range(PASSES):
+            nc.vector.tensor_copy(gw[o][:], xw[:, o, :].indirect(pick[:]))
+
+        yp = [psum.tile([P, S], F32, name="yp%d" % t) for t in range(PACK)]
+        for t0 in (0, 2):
+            for o, t in ((0, t0), (0, t0 + 1), (1, t0), (1, t0 + 1)):
+                nc.tensor.matmul_mx(
+                    out=yp[t][:],
+                    lhsT=w1wd[t][:, o, :].bitcast(FP4X4),
+                    lhsT_scale=w1sd[t][:, o, :],
+                    rhs=gw[o][:].bitcast(FP8X4),
+                    rhs_scale=gs[o][:],
+                    start=(o == 0),
+                    stop=(o == PASSES - 1),
+                )
+
+        y = [sb("y%d" % t, [P, S], F32) for t in range(PACK)]
+        ay = [sb("ay%d" % t, [P, S], F32) for t in range(PACK)]
+        sq = sb("sq", [P, S], F32)
+        ssq = sb("ssq", [P, PACK], F32)
+        c1 = sb("c1", [P, PACK], F32)
+        c2 = sb("c2", [P, PACK], F32)
+        hb0 = sb("hb0", [P, PACK, HALF], BF16)
+        hb1 = sb("hb1", [P, 2, PACK, QUARTER], BF16)
+
+        def group(name, t0, lo, n):
+            g = {"t0": t0, "lo": lo, "n": n}
+            for key in ("a", "c", "b", "lo_", "hi", "tt", "mx", "med", "mn", "rng", "q"):
+                g[key] = sb(name + key, [P, 2, n], F32)
+            return g
+
+        def gather(g, key, i, on_vector=False):
+            lst = lists["acb".index(key)]
+            win = y[g["t0"] + i][:].indirect(lst[:, g["lo"] // 16 : (g["lo"] + g["n"]) // 16])
+            if on_vector:
+                nc.vector.tensor_copy(g[key][:, i, :], win)
+            else:
+                nc.scalar.activation(g[key][:, i, :], win, ACT.Copy)
+
+        def gathers(g):
+            for key in "acb":
+                for i in range(2):
+                    gather(g, key, i)
+
+        def order_stats(g):
+            tt = nc.vector.tensor_tensor
+            tt(g["lo_"][:], g["a"][:], g["c"][:], ALU.min)
+            tt(g["hi"][:], g["a"][:], g["c"][:], ALU.max)
+            tt(g["tt"][:], g["lo_"][:], g["b"][:], ALU.max)
+            tt(g["mx"][:], g["hi"][:], g["b"][:], ALU.max)
+            tt(g["med"][:], g["hi"][:], g["tt"][:], ALU.min)
+            tt(g["mn"][:], g["lo_"][:], g["b"][:], ALU.min)
+            tt(g["rng"][:], g["mx"][:], g["mn"][:], ALU.subtract)
+
+        def combine(g):
+            lo, n = g["lo"], g["n"]
+            for i in range(2):
+                t = g["t0"] + i
+                nc.vector.scalar_tensor_tensor(
+                    g["q"][:, i, :], g["med"][:, i, :], c1[:, t : t + 1], ay[t][:, lo : lo + n], ALU.mult, ALU.mult
+                )
+            for i in range(2):
+                t = g["t0"] + i
+                rng, q = g["rng"][:, i, :], g["q"][:, i, :]
+                if lo == 0:
+                    dst = hb0[:, t, :]
+                elif n == HALF:
+                    dst = hb1[:, :, t, :]
+                    rng = rng.rearrange("p (s j) -> p s j", s=2)
+                    q = q.rearrange("p (s j) -> p s j", s=2)
+                else:
+                    dst = hb1[:, (lo - HALF) // QUARTER, t, :]
+                nc.vector.scalar_tensor_tensor(dst, rng, c2[:, t : t + 1], q, ALU.mult, ALU.subtract)
+
+        def finish(name, planes, lo, n):
+            woven = sb(name + "woven", [P, n, PACK], BF16)
+            nc.vector.tensor_copy(
+                woven[:].rearrange("p (c i) t -> p c t i", i=4), planes.rearrange("p t (c i) -> p c t i", i=4)
+            )
+            codes = sb(name + "codes", [P, n], U32)
+            scales = sb(name + "scales", [P, n], U8)
+            nc.vector.quantize_mx(
+                out=codes[:].bitcast(FP8X4), scales=scales[:], in_=woven[:].rearrange("p j t -> p (j t)")
+            )
+            acc = psum.tile([P, n], F32, name=name + "acc")
+            nc.tensor.matmul_mx(
+                out=acc[:],
+                lhsT=w2w[:].bitcast(FP4X4),
+                lhsT_scale=w2s[:, 0, :],
+                rhs=codes[:].bitcast(FP8X4),
+                rhs_scale=scales[:],
+                start=True,
+                stop=True,
+            )
+            res = sb(name + "res", [P, n], F32)
+            nc.scalar.copy(res[:], acc[:])
+            nc.sync.dma_start(out[:, lo : lo + n], res[:])
+
+        g0 = group("g0", 0, 0, HALF)
+        g1 = group("g1", 0, HALF, HALF)
+        g2 = group("g2", 2, 0, HALF)
+        g3 = group("g3", 2, HALF, QUARTER)
+        g4 = group("g4", 2, HALF + QUARTER, QUARTER)
+
+        nc.scalar.copy(y[0][:], yp[0][:])
+        nc.vector.tensor_copy(y[1][:], yp[1][:])
+        for key in "acb":
+            gather(g0, key, 0)
+            gather(g0, key, 1, on_vector=True)
+        gathers(g1)
+        order_stats(g0)
+        for t in range(PACK):
+            nc.scalar.activation(sq[:], yp[t][:], ACT.Square, accum_out=ssq[:, t : t + 1])
+        var = sb("var", [P, PACK], F32)
+        rstd = sb("rstd", [P, PACK], F32)
+        nc.gpsimd.tensor_scalar(var[:], ssq[:], 1.0 / S, 0.1, ALU.mult, ALU.add)
+        nc.gpsimd.tensor_tensor(rstd[:], var[:], expo[:], ALU.pow)
+        nc.gpsimd.tensor_tensor(c2[:], rstd[:], um[:], ALU.mult)
+        nc.gpsimd.tensor_tensor(c1[:], c2[:], rstd[:], ALU.mult)
+        for t in (0, 1):
+            nc.scalar.activation(ay[t][:], yp[t][:], ACT.Abs, scale=2.5)
+        order_stats(g1)
+        for t in (2, 3):
+            nc.scalar.copy(y[t][:], yp[t][:])
+        gathers(g2)
+        combine(g0)
+        combine(g1)
+        for t in (2, 3):
+            nc.scalar.activation(ay[t][:], yp[t][:], ACT.Abs, scale=2.5)
+        order_stats(g2)
+        gathers(g3)
+        gathers(g4)
+        combine(g2)
+        order_stats(g3)
+        finish("f0", hb0[:], 0, HALF)
+        combine(g3)
+        order_stats(g4)
+        finish("f1", hb1[:, 0], HALF, QUARTER)
+        combine(g4)
+        finish("f2", hb1[:, 1], HALF + QUARTER, QUARTER)

@@ -46,34 +46,36 @@ def tile_picked_ygossip_rng_p_kernel(
         w2s = sb("w2s", [P, 1, N], U8)
         nc.vector.memset(xs[:].bitcast(I32), 0)
         nc.gpsimd.memset(w1s[:].bitcast(I32), 0)
-        nc.gpsimd.memset(w2s[:].bitcast(I32), 0)
+        nc.vector.memset(w2s[:].bitcast(I32), 0)
 
-        pick = keep.tile([P, S // 16], U16, name="pick")
-        nc.sync.dma_start(pick[:], offs)
-        w1w = sb("w1w", [P, PASSES, 2 * H], U8)
-        nc.sync.dma_start(w1w[:].bitcast(I32), w1_words.rearrange("o p c -> p o c").bitcast(I32))
-        xw = sb("xw", [P, PASSES, T], U32)
-        nc.sync.dma_start(xw[:].bitcast(I32), x_words.rearrange("o p n t -> p o (n t)").bitcast(I32))
-        load_scale_rows(nc.scalar, xs, x_scales)
-        load_scale_rows(nc.scalar, w1s, w1_scales)
-        lists = []
-        for name, src in (("la", p1), ("lc", p3), ("lb", p2)):
+        def load_list(name, src):
             lst = keep.tile([P, S // 16], U16, name=name)
             nc.sync.dma_start(lst[:], src)
-            lists.append(lst)
+            return lst
+
+        w1w = sb("w1w", [P, PASSES, 2 * H], U8)
+        nc.sync.dma_start(w1w[:].bitcast(I32), w1_words.rearrange("o p c -> p o c").bitcast(I32))
+        xw = [sb("xw%d" % o, [P, T], U32) for o in range(PASSES)]
+        nc.sync.dma_start(xw[0][:].bitcast(I32), x_words[0].rearrange("p n t -> p (n t)").bitcast(I32))
+        pick = load_list("pick", offs)
+        nc.sync.dma_start(xw[1][:].bitcast(I32), x_words[1].rearrange("p n t -> p (n t)").bitcast(I32))
+        lists = [load_list("la", p1), load_list("lc", p3), load_list("lb", p2)]
         u = sb("u", [P, PACK], F32)
-        nc.sync.dma_start(u[:], unit.rearrange("(p t) o -> p (t o)", t=PACK))
+        nc.scalar.dma_start(u[:], unit.rearrange("(p t) o -> p (t o)", t=PACK))
         w2w = sb("w2w", [P, 2 * N], U8)
-        nc.sync.dma_start(w2w[:].bitcast(I32), w2_words[0].bitcast(I32))
+        nc.scalar.dma_start(w2w[:].bitcast(I32), w2_words[0].bitcast(I32))
+        load_scale_rows(nc.scalar, xs, x_scales)
+        load_scale_rows(nc.gpsimd, w1s, w1_scales)
         load_scale_rows(nc.sync, w2s, w2_scales)
 
-        w1wd = [sb("w1wd%d" % t, [P, PASSES, 2 * P], U8) for t in range(PACK)]
+        w1wd = sb("w1wd", [P, PASSES, PACK, 2 * P], U8)
         w1sd = [sb("w1sd%d" % t, [P, PASSES, P], U8) for t in range(PACK)]
-        for t in range(PACK):
-            nc.gpsimd.tensor_copy(
-                w1wd[t][:].rearrange("p o (m b) -> p o m b", b=2),
-                w1w[:].rearrange("p o (m t b) -> p o m t b", t=PACK, b=2)[:, :, :, t, :],
+        for o in range(PASSES):
+            nc.vector.tensor_copy(
+                w1wd[:, o].rearrange("p t (m b) -> p t m b", b=2),
+                w1w[:, o].rearrange("p (m t b) -> p t m b", t=PACK, b=2),
             )
+        for t in range(PACK):
             nc.gpsimd.tensor_copy(w1sd[t][:], w1s[:].rearrange("p o (m t) -> p o m t", t=PACK)[:, :, :, t])
         um = sb("um", [P, PACK], F32)
         nc.gpsimd.tensor_scalar(um[:], u[:], -0.4, 0.0, ALU.mult, ALU.add)
@@ -83,86 +85,112 @@ def tile_picked_ygossip_rng_p_kernel(
         gw = [sb("gw%d" % o, [P, S], U32) for o in range(PASSES)]
         gs = [sb("gs%d" % o, [P, S], U8) for o in range(PASSES)]
         for o in range(PASSES):
-            nc.vector.tensor_copy(gs[o][:], xs[:, o, :].indirect(pick[:]))
-        for o in range(PASSES):
-            nc.vector.tensor_copy(gw[o][:], xw[:, o, :].indirect(pick[:]))
+            nc.vector.tensor_copy(gw[o][:], xw[o][:].indirect(pick[:]))
+        nc.vector.tensor_copy(gs[0][:], xs[:, 0, :].indirect(pick[:]))
+        halves = (slice(0, HALF), slice(HALF, S))
+        for h in range(2):
+            nc.vector.tensor_copy(gs[1][:, halves[h]], xs[:, 1, :].indirect(pick[:, 16 * h : 16 * (h + 1)]))
 
-        yp = [psum.tile([P, S], F32, name="yp%d" % t) for t in range(PACK)]
-        for t0 in (0, 2):
-            for o, t in ((0, t0), (0, t0 + 1), (1, t0), (1, t0 + 1)):
-                nc.tensor.matmul_mx(
-                    out=yp[t][:],
-                    lhsT=w1wd[t][:, o, :].bitcast(FP4X4),
-                    lhsT_scale=w1sd[t][:, o, :],
-                    rhs=gw[o][:].bitcast(FP8X4),
-                    rhs_scale=gs[o][:],
-                    start=(o == 0),
-                    stop=(o == PASSES - 1),
-                )
+        def product(acc, t, o, cols):
+            nc.tensor.matmul_mx(
+                out=acc[:],
+                lhsT=w1wd[:, o, t, :].bitcast(FP4X4),
+                lhsT_scale=w1sd[t][:, o, :],
+                rhs=gw[o][:, cols].bitcast(FP8X4),
+                rhs_scale=gs[o][:, cols],
+                start=(o == 0),
+                stop=(o == PASSES - 1),
+            )
+
+        yp0 = [psum.tile([P, HALF], F32, name="yp0%d" % h) for h in range(2)]
+        yp = [None] + [psum.tile([P, S], F32, name="yp%d" % t) for t in range(1, PACK)]
+        for o in range(PASSES):
+            for h in range(2):
+                product(yp0[h], 0, o, halves[h])
+        for t in range(1, PACK):
+            for o in range(PASSES):
+                product(yp[t], t, o, slice(0, S))
 
         y = [sb("y%d" % t, [P, S], F32) for t in range(PACK)]
         ay = [sb("ay%d" % t, [P, S], F32) for t in range(PACK)]
         sq = sb("sq", [P, S], F32)
         ssq = sb("ssq", [P, PACK], F32)
+        var = sb("var", [P, PACK], F32)
+        rstd = sb("rstd", [P, PACK], F32)
         c1 = sb("c1", [P, PACK], F32)
         c2 = sb("c2", [P, PACK], F32)
-        hb0 = sb("hb0", [P, PACK, HALF], BF16)
-        hb1 = sb("hb1", [P, 2, PACK, QUARTER], BF16)
+        hb = sb("hb", [P, 4, PACK, QUARTER], BF16)
 
-        def group(name, t0, lo, n):
-            g = {"t0": t0, "lo": lo, "n": n}
-            for key in ("a", "c", "b", "lo_", "hi", "tt", "mx", "med", "mn", "rng", "q"):
-                g[key] = sb(name + key, [P, 2, n], F32)
+        def group(name, pieces):
+            n = sum(piece[2] for piece in pieces)
+            g = {"pieces": pieces}
+            for key in ("a", "c", "b", "lo", "hi", "tt", "mx", "med", "mn", "rng", "q"):
+                g[key] = sb(name + key, [P, n], F32)
             return g
 
         def gather(g, key, i, on_vector=False):
+            t, lo, n = g["pieces"][i]
+            at = sum(piece[2] for piece in g["pieces"][:i])
             lst = lists["acb".index(key)]
-            win = y[g["t0"] + i][:].indirect(lst[:, g["lo"] // 16 : (g["lo"] + g["n"]) // 16])
+            win = y[t][:].indirect(lst[:, lo // 16 : (lo + n) // 16])
             if on_vector:
-                nc.vector.tensor_copy(g[key][:, i, :], win)
+                nc.vector.tensor_copy(g[key][:, at : at + n], win)
             else:
-                nc.scalar.activation(g[key][:, i, :], win, ACT.Copy)
+                nc.scalar.activation(g[key][:, at : at + n], win, ACT.Copy)
 
         def gathers(g):
             for key in "acb":
-                for i in range(2):
+                for i in range(len(g["pieces"])):
                     gather(g, key, i)
 
-        def order_stats(g):
+        def order_stats(whole, cols=slice(None)):
+            g = {key: whole[key][:, cols] for key in whole if key != "pieces"}
             tt = nc.vector.tensor_tensor
-            tt(g["lo_"][:], g["a"][:], g["c"][:], ALU.min)
-            tt(g["hi"][:], g["a"][:], g["c"][:], ALU.max)
-            tt(g["tt"][:], g["lo_"][:], g["b"][:], ALU.max)
-            tt(g["mx"][:], g["hi"][:], g["b"][:], ALU.max)
-            tt(g["med"][:], g["hi"][:], g["tt"][:], ALU.min)
-            tt(g["mn"][:], g["lo_"][:], g["b"][:], ALU.min)
-            tt(g["rng"][:], g["mx"][:], g["mn"][:], ALU.subtract)
+            tt(g["lo"], g["a"], g["c"], ALU.min)
+            tt(g["hi"], g["a"], g["c"], ALU.max)
+            tt(g["tt"], g["lo"], g["b"], ALU.max)
+            tt(g["mx"], g["hi"], g["b"], ALU.max)
+            tt(g["med"], g["hi"], g["tt"], ALU.min)
+            tt(g["mn"], g["lo"], g["b"], ALU.min)
+            tt(g["rng"], g["mx"], g["mn"], ALU.subtract)
 
-        def combine(g):
-            lo, n = g["lo"], g["n"]
-            for i in range(2):
-                t = g["t0"] + i
+        def combine(found):
+            for g, at, t, lo, n in found:
                 nc.vector.scalar_tensor_tensor(
-                    g["q"][:, i, :], g["med"][:, i, :], c1[:, t : t + 1], ay[t][:, lo : lo + n], ALU.mult, ALU.mult
+                    g["q"][:, at : at + n], g["med"][:, at : at + n], c1[:, t : t + 1], ay[t][:, lo : lo + n],
+                    ALU.mult, ALU.mult,
                 )
-            for i in range(2):
-                t = g["t0"] + i
-                rng, q = g["rng"][:, i, :], g["q"][:, i, :]
-                if lo == 0:
-                    dst = hb0[:, t, :]
-                elif n == HALF:
-                    dst = hb1[:, :, t, :]
-                    rng = rng.rearrange("p (s j) -> p s j", s=2)
-                    q = q.rearrange("p (s j) -> p s j", s=2)
-                else:
-                    dst = hb1[:, (lo - HALF) // QUARTER, t, :]
-                nc.vector.scalar_tensor_tensor(dst, rng, c2[:, t : t + 1], q, ALU.mult, ALU.subtract)
+            for g, at, t, lo, n in found:
+                nc.vector.scalar_tensor_tensor(
+                    hb[:, lo // QUARTER : (lo + n) // QUARTER, t, :],
+                    g["rng"][:, at : at + n].rearrange("p (s j) -> p s j", j=QUARTER),
+                    c2[:, t : t + 1],
+                    g["q"][:, at : at + n].rearrange("p (s j) -> p s j", j=QUARTER),
+                    ALU.mult, ALU.subtract,
+                )
 
-        def finish(name, planes, lo, n):
+        def coefficients(t0):
+            pair = slice(t0, t0 + 2)
+            for t in (t0, t0 + 1):
+                nc.scalar.activation(sq[:], y[t][:], ACT.Square, accum_out=ssq[:, t : t + 1])
+            nc.gpsimd.tensor_scalar(var[:, pair], ssq[:, pair], 1.0 / S, 0.1, ALU.mult, ALU.add)
+            nc.gpsimd.tensor_tensor(rstd[:, pair], var[:, pair], expo[:, pair], ALU.pow)
+            nc.gpsimd.tensor_tensor(c2[:, pair], rstd[:, pair], um[:, pair], ALU.mult)
+            nc.gpsimd.tensor_tensor(c1[:, pair], c2[:, pair], rstd[:, pair], ALU.mult)
+            for t in (t0, t0 + 1):
+                nc.scalar.activation(ay[t][:], y[t][:], ACT.Abs, scale=2.5)
+
+        def finish(name, quarters, on_vector):
+            n = QUARTER * len(quarters)
+            lo = QUARTER * quarters[0]
             woven = sb(name + "woven", [P, n, PACK], BF16)
-            nc.vector.tensor_copy(
-                woven[:].rearrange("p (c i) t -> p c t i", i=4), planes.rearrange("p t (c i) -> p c t i", i=4)
-            )
+            for s in quarters:
+                dst = woven[:, QUARTER * s - lo : QUARTER * (s + 1) - lo, :].rearrange("p (c i) t -> p c t i", i=4)
+                src = hb[:, s].rearrange("p t (c i) -> p c t i", i=4)
+                if on_vector:
+                    nc.vector.tensor_copy(dst, src)
+                else:
+                    nc.scalar.copy(dst, src)
             codes = sb(name + "codes", [P, n], U32)
             scales = sb(name + "scales", [P, n], U8)
             nc.vector.quantize_mx(
@@ -182,45 +210,36 @@ def tile_picked_ygossip_rng_p_kernel(
             nc.scalar.copy(res[:], acc[:])
             nc.sync.dma_start(out[:, lo : lo + n], res[:])
 
-        g0 = group("g0", 0, 0, HALF)
-        g1 = group("g1", 0, HALF, HALF)
-        g2 = group("g2", 2, 0, HALF)
-        g3 = group("g3", 2, HALF, QUARTER)
-        g4 = group("g4", 2, HALF + QUARTER, QUARTER)
+        ga = group("ga", [(0, 0, HALF), (0, HALF, HALF)])
+        gc = group("gc", [(1, 0, HALF), (1, HALF, HALF)])
+        gd = group("gd", [(2, 0, HALF), (3, 0, HALF)])
+        ge = group("ge", [(2, HALF, HALF), (3, HALF, HALF)])
 
-        nc.scalar.copy(y[0][:], yp[0][:])
+        nc.scalar.copy(y[0][:, halves[0]], yp0[0][:])
+        nc.vector.tensor_copy(y[0][:, halves[1]], yp0[1][:])
+        gather(ga, "a", 0)
+        gather(ga, "c", 0, on_vector=True)
+        gather(ga, "b", 0)
         nc.vector.tensor_copy(y[1][:], yp[1][:])
         for key in "acb":
-            gather(g0, key, 0)
-            gather(g0, key, 1, on_vector=True)
-        gathers(g1)
-        order_stats(g0)
-        for t in range(PACK):
-            nc.scalar.activation(sq[:], yp[t][:], ACT.Square, accum_out=ssq[:, t : t + 1])
-        var = sb("var", [P, PACK], F32)
-        rstd = sb("rstd", [P, PACK], F32)
-        nc.gpsimd.tensor_scalar(var[:], ssq[:], 1.0 / S, 0.1, ALU.mult, ALU.add)
-        nc.gpsimd.tensor_tensor(rstd[:], var[:], expo[:], ALU.pow)
-        nc.gpsimd.tensor_tensor(c2[:], rstd[:], um[:], ALU.mult)
-        nc.gpsimd.tensor_tensor(c1[:], c2[:], rstd[:], ALU.mult)
-        for t in (0, 1):
-            nc.scalar.activation(ay[t][:], yp[t][:], ACT.Abs, scale=2.5)
-        order_stats(g1)
-        for t in (2, 3):
-            nc.scalar.copy(y[t][:], yp[t][:])
-        gathers(g2)
-        combine(g0)
-        combine(g1)
-        for t in (2, 3):
-            nc.scalar.activation(ay[t][:], yp[t][:], ACT.Abs, scale=2.5)
-        order_stats(g2)
-        gathers(g3)
-        gathers(g4)
-        combine(g2)
-        order_stats(g3)
-        finish("f0", hb0[:], 0, HALF)
-        combine(g3)
-        order_stats(g4)
-        finish("f1", hb1[:, 0], HALF, QUARTER)
-        combine(g4)
-        finish("f2", hb1[:, 1], HALF + QUARTER, QUARTER)
+            gather(ga, key, 1)
+        order_stats(ga, slice(0, HALF))
+        gathers(gc)
+        order_stats(ga, slice(HALF, S))
+        coefficients(0)
+        order_stats(gc)
+        nc.scalar.copy(y[2][:], yp[2][:])
+        nc.vector.tensor_copy(y[3][:], yp[3][:])
+        for key, i in (("a", 0), ("c", 0), ("a", 1), ("c", 1), ("b", 0), ("b", 1)):
+            gather(gd, key, i)
+        combine([(ga, 0, 0, 0, S), (gc, 0, 1, 0, S)])
+        coefficients(2)
+        order_stats(gd)
+        gathers(ge)
+        combine([(gd, 0, 2, 0, HALF), (gd, HALF, 3, 0, HALF)])
+        order_stats(ge)
+        finish("f0", [0, 1], False)
+        combine([(ge, 0, 2, HALF, QUARTER), (ge, HALF, 3, HALF, QUARTER)])
+        finish("f1", [2], False)
+        combine([(ge, QUARTER, 2, HALF + QUARTER, QUARTER), (ge, HALF + QUARTER, 3, HALF + QUARTER, QUARTER)])
+        finish("f2", [3], True)

@@ -31,8 +31,8 @@ def tile_picked_ygossip_rng_p_kernel(
         keep = ctx.enter_context(tc.tile_pool(name="keep", bufs=1))
         psum = ctx.enter_context(tc.psum_pool(name="psum", bufs=1))
 
-        def sb(name, shape, dtype):
-            return keep.tile(shape, dtype, name=name, align_bytes=64)
+        def sb(name, shape, dtype, tag=None):
+            return keep.tile(shape, dtype, name=name, tag=tag or name, align_bytes=64)
 
         def load_scale_rows(queue, plane, rows):
             for q in range(4):
@@ -61,31 +61,30 @@ def tile_picked_ygossip_rng_p_kernel(
         nc.sync.dma_start(xw[1][:].bitcast(I32), x_words[1].rearrange("p n t -> p (n t)").bitcast(I32))
         lists = [load_list("la", p1), load_list("lc", p3), load_list("lb", p2)]
         u = sb("u", [P, PACK], F32)
-        nc.scalar.dma_start(u[:], unit.rearrange("(p t) o -> p (t o)", t=PACK))
+        nc.gpsimd.dma_start(u[:], unit.rearrange("(p t) o -> p (t o)", t=PACK))
         w2w = sb("w2w", [P, 2 * N], U8)
-        nc.scalar.dma_start(w2w[:].bitcast(I32), w2_words[0].bitcast(I32))
+        nc.gpsimd.dma_start(w2w[:].bitcast(I32), w2_words[0].bitcast(I32))
+        load_scale_rows(nc.scalar, w1s, w1_scales)
         load_scale_rows(nc.scalar, xs, x_scales)
-        load_scale_rows(nc.gpsimd, w1s, w1_scales)
         load_scale_rows(nc.sync, w2s, w2_scales)
 
         w1wd = sb("w1wd", [P, PASSES, PACK, 2 * P], U8)
-        w1sd = [sb("w1sd%d" % t, [P, PASSES, P], U8) for t in range(PACK)]
+        w1sd = sb("w1sd", [P, PASSES, PACK, P], U8)
         for o in range(PASSES):
             nc.vector.tensor_copy(
                 w1wd[:, o].rearrange("p t (m b) -> p t m b", b=2),
                 w1w[:, o].rearrange("p (m t b) -> p t m b", t=PACK, b=2),
             )
-        for t in range(PACK):
-            nc.gpsimd.tensor_copy(w1sd[t][:], w1s[:].rearrange("p o (m t) -> p o m t", t=PACK)[:, :, :, t])
         um = sb("um", [P, PACK], F32)
-        nc.gpsimd.tensor_scalar(um[:], u[:], -0.4, 0.0, ALU.mult, ALU.add)
-        expo = sb("expo", [P, PACK], F32)
-        nc.gpsimd.memset(expo[:], -0.5)
+        nc.gpsimd.tensor_scalar(um[:], u[:], -0.16, 0.0, ALU.mult, ALU.add)
+        warm = sb("warm", [P, 1], F32)
+        nc.scalar.activation(warm[:], u[:, 0:1], ACT.Abs_reciprocal_sqrt, bias=0.016, scale=0.16 / S)
 
         gw = [sb("gw%d" % o, [P, S], U32) for o in range(PASSES)]
         gs = [sb("gs%d" % o, [P, S], U8) for o in range(PASSES)]
         for o in range(PASSES):
             nc.vector.tensor_copy(gw[o][:], xw[o][:].indirect(pick[:]))
+        nc.vector.tensor_copy(w1sd[:], w1s[:].rearrange("p o (m t) -> p o t m", t=PACK))
         nc.vector.tensor_copy(gs[0][:], xs[:, 0, :].indirect(pick[:]))
         halves = (slice(0, HALF), slice(HALF, S))
         for h in range(2):
@@ -95,7 +94,7 @@ def tile_picked_ygossip_rng_p_kernel(
             nc.tensor.matmul_mx(
                 out=acc[:],
                 lhsT=w1wd[:, o, t, :].bitcast(FP4X4),
-                lhsT_scale=w1sd[t][:, o, :],
+                lhsT_scale=w1sd[:, o, t, :],
                 rhs=gw[o][:, cols].bitcast(FP8X4),
                 rhs_scale=gs[o][:, cols],
                 start=(o == 0),
@@ -115,17 +114,15 @@ def tile_picked_ygossip_rng_p_kernel(
         ay = [sb("ay%d" % t, [P, S], F32) for t in range(PACK)]
         sq = sb("sq", [P, S], F32)
         ssq = sb("ssq", [P, PACK], F32)
-        var = sb("var", [P, PACK], F32)
         rstd = sb("rstd", [P, PACK], F32)
-        c1 = sb("c1", [P, PACK], F32)
         c2 = sb("c2", [P, PACK], F32)
         hb = sb("hb", [P, 4, PACK, QUARTER], BF16)
 
-        def group(name, pieces):
+        def group(name, pieces, reuse=None):
             n = sum(piece[2] for piece in pieces)
             g = {"pieces": pieces}
             for key in ("a", "c", "b", "lo", "hi", "tt", "mx", "med", "mn", "rng", "q"):
-                g[key] = sb(name + key, [P, n], F32)
+                g[key] = sb(name + key, [P, n], F32, reuse if key == "c" else None)
             return g
 
         def gather(g, key, i, on_vector=False):
@@ -157,7 +154,7 @@ def tile_picked_ygossip_rng_p_kernel(
         def combine(found):
             for g, at, t, lo, n in found:
                 nc.vector.scalar_tensor_tensor(
-                    g["q"][:, at : at + n], g["med"][:, at : at + n], c1[:, t : t + 1], ay[t][:, lo : lo + n],
+                    g["q"][:, at : at + n], g["med"][:, at : at + n], c2[:, t : t + 1], ay[t][:, lo : lo + n],
                     ALU.mult, ALU.mult,
                 )
             for g, at, t, lo, n in found:
@@ -173,14 +170,14 @@ def tile_picked_ygossip_rng_p_kernel(
             pair = slice(t0, t0 + 2)
             for t in (t0, t0 + 1):
                 nc.scalar.activation(sq[:], y[t][:], ACT.Square, accum_out=ssq[:, t : t + 1])
-            nc.gpsimd.tensor_scalar(var[:, pair], ssq[:, pair], 1.0 / S, 0.1, ALU.mult, ALU.add)
-            nc.gpsimd.tensor_tensor(rstd[:, pair], var[:, pair], expo[:, pair], ALU.pow)
-            nc.gpsimd.tensor_tensor(c2[:, pair], rstd[:, pair], um[:, pair], ALU.mult)
-            nc.gpsimd.tensor_tensor(c1[:, pair], c2[:, pair], rstd[:, pair], ALU.mult)
+            nc.scalar.activation(
+                rstd[:, pair], ssq[:, pair], ACT.Abs_reciprocal_sqrt, bias=0.016, scale=0.16 / S
+            )
             for t in (t0, t0 + 1):
-                nc.scalar.activation(ay[t][:], y[t][:], ACT.Abs, scale=2.5)
+                nc.scalar.activation(c2[:, t : t + 1], rstd[:, t : t + 1], ACT.Copy, scale=um[:, t : t + 1])
+                nc.scalar.activation(ay[t][:], y[t][:], ACT.Abs, scale=rstd[:, t : t + 1])
 
-        def finish(name, quarters, on_vector):
+        def finish(name, quarters, on_vector, reuse):
             n = QUARTER * len(quarters)
             lo = QUARTER * quarters[0]
             woven = sb(name + "woven", [P, n, PACK], BF16)
@@ -191,7 +188,7 @@ def tile_picked_ygossip_rng_p_kernel(
                     nc.vector.tensor_copy(dst, src)
                 else:
                     nc.scalar.copy(dst, src)
-            codes = sb(name + "codes", [P, n], U32)
+            codes = sb(name + "codes", [P, n], U32, reuse)
             scales = sb(name + "scales", [P, n], U8)
             nc.vector.quantize_mx(
                 out=codes[:].bitcast(FP8X4), scales=scales[:], in_=woven[:].rearrange("p j t -> p (j t)")
@@ -212,7 +209,7 @@ def tile_picked_ygossip_rng_p_kernel(
 
         ga = group("ga", [(0, 0, HALF), (0, HALF, HALF)])
         gc = group("gc", [(1, 0, HALF), (1, HALF, HALF)])
-        gd = group("gd", [(2, 0, HALF), (3, 0, HALF)])
+        gd = group("gd", [(2, 0, HALF), (3, 0, HALF)], "gcmn")
         ge = group("ge", [(2, HALF, HALF), (3, HALF, HALF)])
 
         nc.scalar.copy(y[0][:, halves[0]], yp0[0][:])
@@ -220,26 +217,28 @@ def tile_picked_ygossip_rng_p_kernel(
         gather(ga, "a", 0)
         gather(ga, "c", 0, on_vector=True)
         gather(ga, "b", 0)
-        nc.vector.tensor_copy(y[1][:], yp[1][:])
-        for key in "acb":
-            gather(ga, key, 1)
+        gather(ga, "c", 1, on_vector=True)
+        nc.scalar.copy(y[1][:], yp[1][:])
+        gather(ga, "a", 1)
+        gather(ga, "b", 1)
         order_stats(ga, slice(0, HALF))
         gathers(gc)
         order_stats(ga, slice(HALF, S))
         coefficients(0)
+        for t in (2, 3):
+            nc.scalar.copy(y[t][:], yp[t][:])
         order_stats(gc)
-        nc.scalar.copy(y[2][:], yp[2][:])
-        nc.vector.tensor_copy(y[3][:], yp[3][:])
-        for key, i in (("a", 0), ("c", 0), ("a", 1), ("c", 1), ("b", 0), ("b", 1)):
-            gather(gd, key, i)
         combine([(ga, 0, 0, 0, S), (gc, 0, 1, 0, S)])
+        for key in "acb":
+            for i in range(2):
+                gather(gd, key, i, on_vector=(key == "c"))
         coefficients(2)
         order_stats(gd)
         gathers(ge)
         combine([(gd, 0, 2, 0, HALF), (gd, HALF, 3, 0, HALF)])
         order_stats(ge)
-        finish("f0", [0, 1], False)
+        finish("f0", [0, 1], False, "gemn")
         combine([(ge, 0, 2, HALF, QUARTER), (ge, HALF, 3, HALF, QUARTER)])
-        finish("f1", [2], False)
+        finish("f1", [2], False, None)
         combine([(ge, QUARTER, 2, HALF + QUARTER, QUARTER), (ge, HALF + QUARTER, 3, HALF + QUARTER, QUARTER)])
-        finish("f2", [3], True)
+        finish("f2", [3], True, None)

@@ -19,8 +19,11 @@ ACT = mybir.ActivationFunctionType
 P = 128
 PACK = 4
 PASSES = K // (P * PACK)
+PER_COLUMN = 16
 HALF = S // 2
 QUARTER = S // 4
+RUN = 4
+EPS, RANGE_WEIGHT = 0.1, 0.4
 
 
 def tile_picked_ygossip_rng_p_kernel(
@@ -34,24 +37,27 @@ def tile_picked_ygossip_rng_p_kernel(
         def sb(name, shape, dtype, tag=None):
             return keep.tile(shape, dtype, name=name, tag=tag or name, align_bytes=64)
 
-        def load_scale_rows(queue, plane, rows):
+        def load_scale_rows(queue, scale_tile, rows):
             for q in range(4):
                 queue.dma_start(
-                    plane[32 * q : 32 * q + 4].bitcast(I32),
+                    scale_tile[32 * q : 32 * q + 4].bitcast(I32),
                     rows[:, 4 * q : 4 * q + 4, :].rearrange("o r c -> r o c").bitcast(I32),
                 )
+
+        def load_list(name, src):
+            lst = keep.tile([P, S // PER_COLUMN], U16, name=name)
+            nc.sync.dma_start(lst[:], src)
+            return lst
+
+        def entries(lst, first, count):
+            return lst[:, first // PER_COLUMN : (first + count) // PER_COLUMN]
 
         xs = sb("xs", [P, PASSES, T], U8)
         w1s = sb("w1s", [P, PASSES, H], U8)
         w2s = sb("w2s", [P, 1, N], U8)
-        nc.vector.memset(xs[:].bitcast(I32), 0)
-        nc.gpsimd.memset(w1s[:].bitcast(I32), 0)
+        nc.gpsimd.memset(xs[:].bitcast(I32), 0)
+        nc.vector.memset(w1s[:].bitcast(I32), 0)
         nc.vector.memset(w2s[:].bitcast(I32), 0)
-
-        def load_list(name, src):
-            lst = keep.tile([P, S // 16], U16, name=name)
-            nc.sync.dma_start(lst[:], src)
-            return lst
 
         w1w = sb("w1w", [P, PASSES, 2 * H], U8)
         nc.sync.dma_start(w1w[:].bitcast(I32), w1_words.rearrange("o p c -> p o c").bitcast(I32))
@@ -59,42 +65,44 @@ def tile_picked_ygossip_rng_p_kernel(
         nc.sync.dma_start(xw[0][:].bitcast(I32), x_words[0].rearrange("p n t -> p (n t)").bitcast(I32))
         pick = load_list("pick", offs)
         nc.sync.dma_start(xw[1][:].bitcast(I32), x_words[1].rearrange("p n t -> p (n t)").bitcast(I32))
-        lists = [load_list("la", p1), load_list("lc", p3), load_list("lb", p2)]
+        partners = {"a": load_list("la", p1), "c": load_list("lc", p3), "b": load_list("lb", p2)}
         u = sb("u", [P, PACK], F32)
-        nc.gpsimd.dma_start(u[:], unit.rearrange("(p t) o -> p (t o)", t=PACK))
+        nc.scalar.dma_start(u[:], unit.rearrange("(p t) o -> p (t o)", t=PACK))
         w2w = sb("w2w", [P, 2 * N], U8)
         nc.gpsimd.dma_start(w2w[:].bitcast(I32), w2_words[0].bitcast(I32))
-        load_scale_rows(nc.scalar, w1s, w1_scales)
         load_scale_rows(nc.scalar, xs, x_scales)
+        load_scale_rows(nc.scalar, w1s, w1_scales)
         load_scale_rows(nc.sync, w2s, w2_scales)
 
         w1wd = sb("w1wd", [P, PASSES, PACK, 2 * P], U8)
-        w1sd = sb("w1sd", [P, PASSES, PACK, P], U8)
+        w1sd = [sb("w1sd%d" % t, [P, PASSES, P], U8) for t in range(PACK)]
         for o in range(PASSES):
             nc.vector.tensor_copy(
                 w1wd[:, o].rearrange("p t (m b) -> p t m b", b=2),
                 w1w[:, o].rearrange("p (m t b) -> p t m b", t=PACK, b=2),
             )
+        for t in range(PACK):
+            nc.gpsimd.tensor_copy(w1sd[t][:], w1s[:].rearrange("p o (m t) -> p o m t", t=PACK)[:, :, :, t])
         um = sb("um", [P, PACK], F32)
-        nc.gpsimd.tensor_scalar(um[:], u[:], -0.16, 0.0, ALU.mult, ALU.add)
+        nc.gpsimd.tensor_scalar(um[:], u[:], -(RANGE_WEIGHT**2), 0.0, ALU.mult, ALU.add)
+        rstd_scale, rstd_bias = RANGE_WEIGHT**2 / S, RANGE_WEIGHT**2 * EPS
         warm = sb("warm", [P, 1], F32)
-        nc.scalar.activation(warm[:], u[:, 0:1], ACT.Abs_reciprocal_sqrt, bias=0.016, scale=0.16 / S)
+        nc.scalar.activation(warm[:], u[:, 0:1], ACT.Abs_reciprocal_sqrt, bias=rstd_bias, scale=rstd_scale)
 
         gw = [sb("gw%d" % o, [P, S], U32) for o in range(PASSES)]
         gs = [sb("gs%d" % o, [P, S], U8) for o in range(PASSES)]
         for o in range(PASSES):
             nc.vector.tensor_copy(gw[o][:], xw[o][:].indirect(pick[:]))
-        nc.vector.tensor_copy(w1sd[:], w1s[:].rearrange("p o (m t) -> p o t m", t=PACK))
         nc.vector.tensor_copy(gs[0][:], xs[:, 0, :].indirect(pick[:]))
         halves = (slice(0, HALF), slice(HALF, S))
         for h in range(2):
-            nc.vector.tensor_copy(gs[1][:, halves[h]], xs[:, 1, :].indirect(pick[:, 16 * h : 16 * (h + 1)]))
+            nc.vector.tensor_copy(gs[1][:, halves[h]], xs[:, 1, :].indirect(entries(pick, h * HALF, HALF)))
 
-        def product(acc, t, o, cols):
+        def first_product(acc, t, o, cols):
             nc.tensor.matmul_mx(
                 out=acc[:],
                 lhsT=w1wd[:, o, t, :].bitcast(FP4X4),
-                lhsT_scale=w1sd[:, o, t, :],
+                lhsT_scale=w1sd[t][:, o, :],
                 rhs=gw[o][:, cols].bitcast(FP8X4),
                 rhs_scale=gs[o][:, cols],
                 start=(o == 0),
@@ -102,93 +110,92 @@ def tile_picked_ygossip_rng_p_kernel(
             )
 
         yp0 = [psum.tile([P, HALF], F32, name="yp0%d" % h) for h in range(2)]
-        yp = [None] + [psum.tile([P, S], F32, name="yp%d" % t) for t in range(1, PACK)]
+        yp = {t: psum.tile([P, S], F32, name="yp%d" % t) for t in range(1, PACK)}
         for o in range(PASSES):
             for h in range(2):
-                product(yp0[h], 0, o, halves[h])
+                first_product(yp0[h], 0, o, halves[h])
         for t in range(1, PACK):
             for o in range(PASSES):
-                product(yp[t], t, o, slice(0, S))
+                first_product(yp[t], t, o, slice(0, S))
 
         y = [sb("y%d" % t, [P, S], F32) for t in range(PACK)]
         ay = [sb("ay%d" % t, [P, S], F32) for t in range(PACK)]
-        sq = sb("sq", [P, S], F32)
+        squares = sb("squares", [P, S], F32)
         ssq = sb("ssq", [P, PACK], F32)
         rstd = sb("rstd", [P, PACK], F32)
-        c2 = sb("c2", [P, PACK], F32)
-        hb = sb("hb", [P, 4, PACK, QUARTER], BF16)
+        coef = sb("coef", [P, PACK], F32)
+        hid = sb("hid", [P, S // QUARTER, PACK, QUARTER], BF16)
 
-        def group(name, pieces, reuse=None):
-            n = sum(piece[2] for piece in pieces)
+        def group(name, pieces, c_tag=None):
             g = {"pieces": pieces}
-            for key in ("a", "c", "b", "lo", "hi", "tt", "mx", "med", "mn", "rng", "q"):
-                g[key] = sb(name + key, [P, n], F32, reuse if key == "c" else None)
+            for key in ("a", "c", "b", "lo", "hi", "up", "mx", "med", "mn", "rng", "prod"):
+                g[key] = sb(name + key, [P, S], F32, c_tag if key == "c" else None)
             return g
 
-        def gather(g, key, i, on_vector=False):
-            t, lo, n = g["pieces"][i]
-            at = sum(piece[2] for piece in g["pieces"][:i])
-            lst = lists["acb".index(key)]
-            win = y[t][:].indirect(lst[:, lo // 16 : (lo + n) // 16])
-            if on_vector:
-                nc.vector.tensor_copy(g[key][:, at : at + n], win)
-            else:
-                nc.scalar.activation(g[key][:, at : at + n], win, ACT.Copy)
-
-        def gathers(g):
+        def gathers(g, c_on_vector):
             for key in "acb":
-                for i in range(len(g["pieces"])):
-                    gather(g, key, i)
+                for half, (t, first) in zip(halves, g["pieces"]):
+                    picked = y[t][:].indirect(entries(partners[key], first, HALF))
+                    if c_on_vector and key == "c":
+                        nc.vector.tensor_copy(g[key][:, half], picked)
+                    else:
+                        nc.scalar.activation(g[key][:, half], picked, ACT.Copy)
 
-        def order_stats(whole, cols=slice(None)):
-            g = {key: whole[key][:, cols] for key in whole if key != "pieces"}
-            tt = nc.vector.tensor_tensor
-            tt(g["lo"], g["a"], g["c"], ALU.min)
-            tt(g["hi"], g["a"], g["c"], ALU.max)
-            tt(g["tt"], g["lo"], g["b"], ALU.max)
-            tt(g["mx"], g["hi"], g["b"], ALU.max)
-            tt(g["med"], g["hi"], g["tt"], ALU.min)
-            tt(g["mn"], g["lo"], g["b"], ALU.min)
-            tt(g["rng"], g["mx"], g["mn"], ALU.subtract)
+        def order_statistics(g):
+            for dst, in0, in1, op in (
+                ("lo", "a", "c", ALU.min),
+                ("hi", "a", "c", ALU.max),
+                ("up", "lo", "b", ALU.max),
+                ("mx", "hi", "b", ALU.max),
+                ("mn", "lo", "b", ALU.min),
+                ("med", "hi", "up", ALU.min),
+                ("rng", "mx", "mn", ALU.subtract),
+            ):
+                nc.vector.tensor_tensor(g[dst][:], g[in0][:], g[in1][:], op)
 
-        def combine(found):
-            for g, at, t, lo, n in found:
+        def combine(runs):
+            for g, at, t, first, n in runs:
                 nc.vector.scalar_tensor_tensor(
-                    g["q"][:, at : at + n], g["med"][:, at : at + n], c2[:, t : t + 1], ay[t][:, lo : lo + n],
-                    ALU.mult, ALU.mult,
+                    g["prod"][:, at : at + n],
+                    g["med"][:, at : at + n],
+                    coef[:, t : t + 1],
+                    ay[t][:, first : first + n],
+                    ALU.mult,
+                    ALU.mult,
                 )
-            for g, at, t, lo, n in found:
+            for g, at, t, first, n in runs:
                 nc.vector.scalar_tensor_tensor(
-                    hb[:, lo // QUARTER : (lo + n) // QUARTER, t, :],
+                    hid[:, first // QUARTER : (first + n) // QUARTER, t, :],
                     g["rng"][:, at : at + n].rearrange("p (s j) -> p s j", j=QUARTER),
-                    c2[:, t : t + 1],
-                    g["q"][:, at : at + n].rearrange("p (s j) -> p s j", j=QUARTER),
-                    ALU.mult, ALU.subtract,
+                    coef[:, t : t + 1],
+                    g["prod"][:, at : at + n].rearrange("p (s j) -> p s j", j=QUARTER),
+                    ALU.mult,
+                    ALU.subtract,
                 )
 
-        def coefficients(t0):
+        def row_factors(t0):
             pair = slice(t0, t0 + 2)
             for t in (t0, t0 + 1):
-                nc.scalar.activation(sq[:], y[t][:], ACT.Square, accum_out=ssq[:, t : t + 1])
+                nc.scalar.activation(squares[:], y[t][:], ACT.Square, accum_out=ssq[:, t : t + 1])
             nc.scalar.activation(
-                rstd[:, pair], ssq[:, pair], ACT.Abs_reciprocal_sqrt, bias=0.016, scale=0.16 / S
+                rstd[:, pair], ssq[:, pair], ACT.Abs_reciprocal_sqrt, bias=rstd_bias, scale=rstd_scale
             )
             for t in (t0, t0 + 1):
-                nc.scalar.activation(c2[:, t : t + 1], rstd[:, t : t + 1], ACT.Copy, scale=um[:, t : t + 1])
+                nc.scalar.activation(coef[:, t : t + 1], rstd[:, t : t + 1], ACT.Copy, scale=um[:, t : t + 1])
                 nc.scalar.activation(ay[t][:], y[t][:], ACT.Abs, scale=rstd[:, t : t + 1])
 
-        def finish(name, quarters, on_vector, reuse):
+        def second_product(name, quarters, codes_tag=None):
             n = QUARTER * len(quarters)
-            lo = QUARTER * quarters[0]
+            first = QUARTER * quarters[0]
             woven = sb(name + "woven", [P, n, PACK], BF16)
             for s in quarters:
-                dst = woven[:, QUARTER * s - lo : QUARTER * (s + 1) - lo, :].rearrange("p (c i) t -> p c t i", i=4)
-                src = hb[:, s].rearrange("p t (c i) -> p c t i", i=4)
-                if on_vector:
-                    nc.vector.tensor_copy(dst, src)
-                else:
-                    nc.scalar.copy(dst, src)
-            codes = sb(name + "codes", [P, n], U32, reuse)
+                nc.scalar.copy(
+                    woven[:, QUARTER * s - first : QUARTER * (s + 1) - first, :].rearrange(
+                        "p (c i) t -> p c t i", i=RUN
+                    ),
+                    hid[:, s].rearrange("p t (c i) -> p c t i", i=RUN),
+                )
+            codes = sb(name + "codes", [P, n], U32, codes_tag)
             scales = sb(name + "scales", [P, n], U8)
             nc.vector.quantize_mx(
                 out=codes[:].bitcast(FP8X4), scales=scales[:], in_=woven[:].rearrange("p j t -> p (j t)")
@@ -205,40 +212,32 @@ def tile_picked_ygossip_rng_p_kernel(
             )
             res = sb(name + "res", [P, n], F32)
             nc.scalar.copy(res[:], acc[:])
-            nc.sync.dma_start(out[:, lo : lo + n], res[:])
+            nc.sync.dma_start(out[:, first : first + n], res[:])
 
-        ga = group("ga", [(0, 0, HALF), (0, HALF, HALF)])
-        gc = group("gc", [(1, 0, HALF), (1, HALF, HALF)])
-        gd = group("gd", [(2, 0, HALF), (3, 0, HALF)], "gcmn")
-        ge = group("ge", [(2, HALF, HALF), (3, HALF, HALF)])
+        tile0 = group("tile0", [(0, 0), (0, HALF)])
+        tile1 = group("tile1", [(1, 0), (1, HALF)])
+        left = group("left", [(2, 0), (3, 0)], c_tag="tile1mn")
+        right = group("right", [(2, HALF), (3, HALF)])
 
         nc.scalar.copy(y[0][:, halves[0]], yp0[0][:])
         nc.vector.tensor_copy(y[0][:, halves[1]], yp0[1][:])
-        gather(ga, "a", 0)
-        gather(ga, "c", 0, on_vector=True)
-        gather(ga, "b", 0)
-        gather(ga, "c", 1, on_vector=True)
+        gathers(tile0, c_on_vector=True)
         nc.scalar.copy(y[1][:], yp[1][:])
-        gather(ga, "a", 1)
-        gather(ga, "b", 1)
-        order_stats(ga, slice(0, HALF))
-        gathers(gc)
-        order_stats(ga, slice(HALF, S))
-        coefficients(0)
+        gathers(tile1, c_on_vector=False)
+        order_statistics(tile0)
+        row_factors(0)
         for t in (2, 3):
             nc.scalar.copy(y[t][:], yp[t][:])
-        order_stats(gc)
-        combine([(ga, 0, 0, 0, S), (gc, 0, 1, 0, S)])
-        for key in "acb":
-            for i in range(2):
-                gather(gd, key, i, on_vector=(key == "c"))
-        coefficients(2)
-        order_stats(gd)
-        gathers(ge)
-        combine([(gd, 0, 2, 0, HALF), (gd, HALF, 3, 0, HALF)])
-        order_stats(ge)
-        finish("f0", [0, 1], False, "gemn")
-        combine([(ge, 0, 2, HALF, QUARTER), (ge, HALF, 3, HALF, QUARTER)])
-        finish("f1", [2], False, None)
-        combine([(ge, QUARTER, 2, HALF + QUARTER, QUARTER), (ge, HALF + QUARTER, 3, HALF + QUARTER, QUARTER)])
-        finish("f2", [3], True, None)
+        order_statistics(tile1)
+        combine([(tile0, 0, 0, 0, S), (tile1, 0, 1, 0, S)])
+        gathers(left, c_on_vector=True)
+        row_factors(2)
+        order_statistics(left)
+        gathers(right, c_on_vector=False)
+        combine([(left, 0, 2, 0, HALF), (left, HALF, 3, 0, HALF)])
+        order_statistics(right)
+        for at in (0, QUARTER):
+            combine([(right, at, 2, HALF + at, QUARTER), (right, HALF + at, 3, HALF + at, QUARTER)])
+        second_product("out0", [0, 1], codes_tag="rightmn")
+        second_product("out1", [2])
+        second_product("out2", [3])

from contextlib import ExitStack

import concourse.mybir as mybir

K, T, S, N, H = 1024, 1024, 512, 128, 512
FLOPS = 2 * K * H * S + 2 * H * N * S

F32 = mybir.dt.float32
BF16 = mybir.dt.bfloat16
I32 = mybir.dt.int32
U32 = mybir.dt.uint32
U16 = mybir.dt.uint16
U8 = mybir.dt.uint8
FP8X4 = mybir.dt.float8_e4m3fn_x4
FP4X4 = mybir.dt.float4_e2m1fn_x4
ALU = mybir.AluOpType
ACT = mybir.ActivationFunctionType

P = 128
PACK = 4
PASSES = K // (P * PACK)
PER_COLUMN = 16
HALF = S // 2
QUARTER = S // 4
RUN = 4
EPS, RANGE_WEIGHT = 0.1, 0.4


def tile_picked_ygossip_rng_p_kernel(
    tc, x_words, x_scales, w1_words, w1_scales, unit, w2_words, w2_scales, offs, p1, p2, p3, out
):
    nc = tc.nc
    with ExitStack() as ctx:
        keep = ctx.enter_context(tc.tile_pool(name="keep", bufs=1))
        psum = ctx.enter_context(tc.psum_pool(name="psum", bufs=1))

        def sb(name, shape, dtype, tag=None):
            return keep.tile(shape, dtype, name=name, tag=tag or name, align_bytes=64)

        def load_scale_rows(queue, scale_tile, rows):
            for q in range(4):
                queue.dma_start(
                    scale_tile[32 * q : 32 * q + 4].bitcast(I32),
                    rows[:, 4 * q : 4 * q + 4, :].rearrange("o r c -> r o c").bitcast(I32),
                )

        def load_list(name, src):
            lst = keep.tile([P, S // PER_COLUMN], U16, name=name)
            nc.sync.dma_start(lst[:], src)
            return lst

        def entries(lst, first, count):
            return lst[:, first // PER_COLUMN : (first + count) // PER_COLUMN]

        xs = sb("xs", [P, PASSES, T], U8)
        w1s = sb("w1s", [P, PASSES, H], U8)
        w2s = sb("w2s", [P, 1, N], U8)
        nc.gpsimd.memset(xs[:].bitcast(I32), 0)
        nc.vector.memset(w1s[:].bitcast(I32), 0)
        nc.vector.memset(w2s[:].bitcast(I32), 0)

        w1w = sb("w1w", [P, PASSES, 2 * H], U8)
        nc.sync.dma_start(w1w[:].bitcast(I32), w1_words.rearrange("o p c -> p o c").bitcast(I32))
        xw = [sb("xw%d" % o, [P, T], U32) for o in range(PASSES)]
        nc.sync.dma_start(xw[0][:].bitcast(I32), x_words[0].rearrange("p n t -> p (n t)").bitcast(I32))
        pick = load_list("pick", offs)
        nc.sync.dma_start(xw[1][:].bitcast(I32), x_words[1].rearrange("p n t -> p (n t)").bitcast(I32))
        partners = {"a": load_list("la", p1), "c": load_list("lc", p3), "b": load_list("lb", p2)}
        u = sb("u", [P, PACK], F32)
        nc.scalar.dma_start(u[:], unit.rearrange("(p t) o -> p (t o)", t=PACK))
        w2w = sb("w2w", [P, 2 * N], U8)
        nc.gpsimd.dma_start(w2w[:].bitcast(I32), w2_words[0].bitcast(I32))
        load_scale_rows(nc.scalar, xs, x_scales)
        load_scale_rows(nc.scalar, w1s, w1_scales)
        load_scale_rows(nc.sync, w2s, w2_scales)

        w1wd = sb("w1wd", [P, PASSES, PACK, 2 * P], U8)
        w1sd = [sb("w1sd%d" % t, [P, PASSES, P], U8) for t in range(PACK)]
        for o in range(PASSES):
            nc.vector.tensor_copy(
                w1wd[:, o].rearrange("p t (m b) -> p t m b", b=2),
                w1w[:, o].rearrange("p (m t b) -> p t m b", t=PACK, b=2),
            )
        for t in range(PACK):
            nc.gpsimd.tensor_copy(w1sd[t][:], w1s[:].rearrange("p o (m t) -> p o m t", t=PACK)[:, :, :, t])
        um = sb("um", [P, PACK], F32)
        nc.gpsimd.tensor_scalar(um[:], u[:], -(RANGE_WEIGHT**2), 0.0, ALU.mult, ALU.add)
        rstd_scale, rstd_bias = RANGE_WEIGHT**2 / S, RANGE_WEIGHT**2 * EPS
        warm = sb("warm", [P, 1], F32)
        nc.scalar.activation(warm[:], u[:, 0:1], ACT.Abs_reciprocal_sqrt, bias=rstd_bias, scale=rstd_scale)

        gw = [sb("gw%d" % o, [P, S], U32) for o in range(PASSES)]
        gs = [sb("gs%d" % o, [P, S], U8) for o in range(PASSES)]
        for o in range(PASSES):
            nc.vector.tensor_copy(gw[o][:], xw[o][:].indirect(pick[:]))
        nc.vector.tensor_copy(gs[0][:], xs[:, 0, :].indirect(pick[:]))
        halves = (slice(0, HALF), slice(HALF, S))
        for h in range(2):
            nc.vector.tensor_copy(gs[1][:, halves[h]], xs[:, 1, :].indirect(entries(pick, h * HALF, HALF)))

        def first_product(acc, t, o, cols):
            nc.tensor.matmul_mx(
                out=acc[:],
                lhsT=w1wd[:, o, t, :].bitcast(FP4X4),
                lhsT_scale=w1sd[t][:, o, :],
                rhs=gw[o][:, cols].bitcast(FP8X4),
                rhs_scale=gs[o][:, cols],
                start=(o == 0),
                stop=(o == PASSES - 1),
            )

        yp0 = [psum.tile([P, HALF], F32, name="yp0%d" % h) for h in range(2)]
        yp = {t: psum.tile([P, S], F32, name="yp%d" % t) for t in range(1, PACK)}
        for o in range(PASSES):
            for h in range(2):
                first_product(yp0[h], 0, o, halves[h])
        for t in range(1, PACK):
            for o in range(PASSES):
                first_product(yp[t], t, o, slice(0, S))

        y = [sb("y%d" % t, [P, S], F32) for t in range(PACK)]
        ay = [sb("ay%d" % t, [P, S], F32) for t in range(PACK)]
        squares = sb("squares", [P, S], F32)
        ssq = sb("ssq", [P, PACK], F32)
        rstd = sb("rstd", [P, PACK], F32)
        coef = sb("coef", [P, PACK], F32)
        hid = sb("hid", [P, S // QUARTER, PACK, QUARTER], BF16)

        def group(name, pieces, c_tag=None):
            g = {"pieces": pieces}
            for key in ("a", "c", "b", "lo", "hi", "up", "mx", "med", "mn", "rng", "prod"):
                g[key] = sb(name + key, [P, S], F32, c_tag if key == "c" else None)
            return g

        def gathers(g, c_on_vector):
            for key in "acb":
                for half, (t, first) in zip(halves, g["pieces"]):
                    picked = y[t][:].indirect(entries(partners[key], first, HALF))
                    if c_on_vector and key == "c":
                        nc.vector.tensor_copy(g[key][:, half], picked)
                    else:
                        nc.scalar.activation(g[key][:, half], picked, ACT.Copy)

        def order_statistics(g):
            for dst, in0, in1, op in (
                ("lo", "a", "c", ALU.min),
                ("hi", "a", "c", ALU.max),
                ("up", "lo", "b", ALU.max),
                ("mx", "hi", "b", ALU.max),
                ("mn", "lo", "b", ALU.min),
                ("med", "hi", "up", ALU.min),
                ("rng", "mx", "mn", ALU.subtract),
            ):
                nc.vector.tensor_tensor(g[dst][:], g[in0][:], g[in1][:], op)

        def combine(runs):
            for g, at, t, first, n in runs:
                nc.vector.scalar_tensor_tensor(
                    g["prod"][:, at : at + n],
                    g["med"][:, at : at + n],
                    coef[:, t : t + 1],
                    ay[t][:, first : first + n],
                    ALU.mult,
                    ALU.mult,
                )
            for g, at, t, first, n in runs:
                nc.vector.scalar_tensor_tensor(
                    hid[:, first // QUARTER : (first + n) // QUARTER, t, :],
                    g["rng"][:, at : at + n].rearrange("p (s j) -> p s j", j=QUARTER),
                    coef[:, t : t + 1],
                    g["prod"][:, at : at + n].rearrange("p (s j) -> p s j", j=QUARTER),
                    ALU.mult,
                    ALU.subtract,
                )

        def row_factors(t0):
            pair = slice(t0, t0 + 2)
            for t in (t0, t0 + 1):
                nc.scalar.activation(squares[:], y[t][:], ACT.Square, accum_out=ssq[:, t : t + 1])
            nc.scalar.activation(
                rstd[:, pair], ssq[:, pair], ACT.Abs_reciprocal_sqrt, bias=rstd_bias, scale=rstd_scale
            )
            for t in (t0, t0 + 1):
                nc.scalar.activation(coef[:, t : t + 1], rstd[:, t : t + 1], ACT.Copy, scale=um[:, t : t + 1])
                nc.scalar.activation(ay[t][:], y[t][:], ACT.Abs, scale=rstd[:, t : t + 1])

        def second_product(name, quarters, codes_tag=None):
            n = QUARTER * len(quarters)
            first = QUARTER * quarters[0]
            woven = sb(name + "woven", [P, n, PACK], BF16)
            for s in quarters:
                nc.scalar.copy(
                    woven[:, QUARTER * s - first : QUARTER * (s + 1) - first, :].rearrange(
                        "p (c i) t -> p c t i", i=RUN
                    ),
                    hid[:, s].rearrange("p t (c i) -> p c t i", i=RUN),
                )
            codes = sb(name + "codes", [P, n], U32, codes_tag)
            scales = sb(name + "scales", [P, n], U8)
            nc.vector.quantize_mx(
                out=codes[:].bitcast(FP8X4), scales=scales[:], in_=woven[:].rearrange("p j t -> p (j t)")
            )
            acc = psum.tile([P, n], F32, name=name + "acc")
            nc.tensor.matmul_mx(
                out=acc[:],
                lhsT=w2w[:].bitcast(FP4X4),
                lhsT_scale=w2s[:, 0, :],
                rhs=codes[:].bitcast(FP8X4),
                rhs_scale=scales[:],
                start=True,
                stop=True,
            )
            res = sb(name + "res", [P, n], F32)
            nc.scalar.copy(res[:], acc[:])
            nc.sync.dma_start(out[:, first : first + n], res[:])

        tile0 = group("tile0", [(0, 0), (0, HALF)])
        tile1 = group("tile1", [(1, 0), (1, HALF)])
        left = group("left", [(2, 0), (3, 0)], c_tag="tile1mn")
        right = group("right", [(2, HALF), (3, HALF)])

        nc.scalar.copy(y[0][:, halves[0]], yp0[0][:])
        nc.vector.tensor_copy(y[0][:, halves[1]], yp0[1][:])
        gathers(tile0, c_on_vector=True)
        nc.scalar.copy(y[1][:], yp[1][:])
        gathers(tile1, c_on_vector=False)
        order_statistics(tile0)
        row_factors(0)
        for t in (2, 3):
            nc.scalar.copy(y[t][:], yp[t][:])
        order_statistics(tile1)
        combine([(tile0, 0, 0, 0, S), (tile1, 0, 1, 0, S)])
        gathers(left, c_on_vector=True)
        row_factors(2)
        order_statistics(left)
        gathers(right, c_on_vector=False)
        combine([(left, 0, 2, 0, HALF), (left, HALF, 3, 0, HALF)])
        order_statistics(right)
        for at in (0, QUARTER):
            combine([(right, at, 2, HALF + at, QUARTER), (right, HALF + at, 3, HALF + at, QUARTER)])
        second_product("out0", [0, 1], codes_tag="rightmn")
        second_product("out1", [2])
        second_product("out2", [3])
